import numpy as np
import ml_dtypes


def mxq(x, axis, fmt="e4m3"):
    dtype, down = {"e4m3": (ml_dtypes.float8_e4m3fn, 7), "e5m2": (ml_dtypes.float8_e5m2, 14)}[fmt]
    v = np.moveaxis(np.asarray(x, np.float32).astype(ml_dtypes.bfloat16).astype(np.float64), axis, -1)
    blocks = v.reshape(v.shape[:-1] + (-1, 32))
    amax = np.abs(blocks).max(-1, keepdims=True)
    byte = np.maximum(np.where(amax > 0, np.frexp(amax)[1] - 1 + 127, 0) - down, 1)
    scale = np.exp2(byte - 127.0)
    codes = (blocks / scale).astype(np.float32).astype(dtype).astype(np.float64)
    return np.moveaxis((codes * scale).reshape(v.shape), -1, axis)


WIDE = False


def mx_kscale(k):
    if not WIDE:
        return np.ones(k)
    levels = np.array([10, -10, 5, -5, 0])
    if k % 512:
        return np.exp2(np.random.permutation(np.resize(levels, k // 32))).repeat(32)
    a = np.empty((k // 512, 16))
    for p in range(k // 512):
        a[p, :8] = np.random.permutation(np.resize(levels, 8))
        for g in range(8):
            far = levels[np.abs(levels - a[p, g]) >= 10]
            a[p, g + 8] = far[np.random.randint(len(far))]
    return np.exp2(a.ravel()).repeat(32)


def f64(x):
    return np.asarray(x).astype(np.float64)


def split(x):
    m, e = np.frexp(f64(x))
    hi = np.ldexp(np.trunc(16.0 * m) / 16.0, e)
    return hi, f64(x) - hi


def gelu(v):
    return 0.5 * v * (1.0 + np.tanh(np.sqrt(2.0 / np.pi) * (v + 0.044715 * v**3)))


K, M, T = 1024, 512, 1536


def setup_inputs():
    n = np.random.standard_normal
    s = mx_kscale(K)[:, None]
    return {
        "w": (n((K, M)) / np.sqrt(K) / s).astype(np.float32),
        "x": (n((K, T)) * s).astype(np.float32),
        "b": (0.3 * n(512)).astype(np.float32),
    }


def reference(w, x, b):
    w_hi, w_lo = split(w)
    w_hi_, w_lo_ = mxq(w_hi, 0, "e4m3"), mxq(w_lo, 0, "e4m3")
    x_ = mxq(f64(x), 0, "e4m3")
    y = w_hi_.T @ x_ + w_lo_.T @ x_
    return gelu(y + f64(b)[:, None])

@@ -1,0 +1,215 @@
+from contextlib import ExitStack
+
+import concourse.mybir as mybir
+from concourse.masks import make_identity
+
+K, M, T = 1024, 512, 1536
+P = 128
+PACK = 4
+K_PASS = P * PACK
+PASSES = K // K_PASS
+CHUNK = 512
+HALF = 256
+M_TILES = M // P
+HI_MASK = -1048576
+
+FLOPS = 2 * 2 * K * M * T
+
+F32 = mybir.dt.float32
+BF16 = mybir.dt.bfloat16
+I32 = mybir.dt.int32
+U32 = mybir.dt.uint32
+U8 = mybir.dt.uint8
+FP8X4 = mybir.dt.float8_e4m3fn_x4
+ALU = mybir.AluOpType
+GELU = mybir.ActivationFunctionType.Gelu_apprx_tanh
+
+
+def rows_view(raw):
+    return raw.rearrange("p t (c i) -> p c t i", i=4)
+
+
+def packed_view(grouped):
+    return grouped.rearrange("p (c i) t -> p c t i", i=4)
+
+
+def tile_mix_hilo_fm_gelu_kernel(tc, w, x, b, out):
+    nc = tc.nc
+    chunks = T // CHUNK
+
+    with ExitStack() as ctx:
+        keep = ctx.enter_context(tc.tile_pool(name="keep", bufs=1))
+        psum = ctx.enter_context(tc.psum_pool(name="psum", bufs=1))
+        ctx.enter_context(tc.manual_schedule())
+
+        w_raw = []
+        x_raw = {}
+        for kp in range(PASSES):
+            wr = keep.tile([P, PACK, M], F32, name="w_raw%d" % kp, align_bytes=64)
+            w_raw.append(wr)
+
+        def load_x(ch, kp):
+            xr = keep.tile([P, PACK, CHUNK], F32, name="x_raw%d_%d" % (ch, kp), align_bytes=64)
+            nc.sync.dma_start(
+                out=xr[:],
+                in_=x[kp * K_PASS:(kp + 1) * K_PASS, ch * CHUNK:(ch + 1) * CHUNK].rearrange("(p j) t -> p j t", j=PACK),
+            )
+            x_raw[(ch, kp)] = xr
+
+        w_rows = [w[kp * K_PASS:(kp + 1) * K_PASS, :].rearrange("(p j) c -> p j c", j=PACK) for kp in range(PASSES)]
+        nc.sync.dma_start(out=w_raw[0][:, 0:2, :], in_=w_rows[0][:, 0:2, :])
+        nc.sync.dma_start(out=w_raw[0][:, 2:4, :], in_=w_rows[0][:, 2:4, :])
+        load_x(0, 0)
+        nc.sync.dma_start(out=w_raw[1][:], in_=w_rows[1])
+        load_x(0, 1)
+        for ch in range(1, chunks):
+            for kp in range(PASSES):
+                load_x(ch, kp)
+
+        warm = keep.tile([P, 1], F32, name="warm")
+        warm_out = keep.tile([P, 1], F32, name="warm_out")
+        b_rows = keep.tile([P, P], F32, name="b_rows")
+        ident = keep.tile([P, P], F32, name="ident")
+        bias = keep.tile([P, M_TILES], F32, name="bias")
+        nc.vector.memset(warm[:], 0.0)
+        nc.gpsimd.memset(b_rows[:], 0.0)
+        make_identity(nc, ident[:])
+        nc.scalar.activation(out=warm_out[:], in_=warm[:], func=GELU)
+        nc.scalar.dma_start(out=b_rows[0:M_TILES, :], in_=b.rearrange("(m p) -> m p", p=P))
+        bT = psum.tile([P, CHUNK], F32, name="bT", tag="acc7")
+        nc.tensor.transpose(bT[:, 0:P], b_rows[:], ident[:])
+
+        hi_f = [keep.tile([P, PACK, M], F32, name="hi_f%d" % kp, align_bytes=64) for kp in range(PASSES)]
+        w_grp = {}
+        w_codes = {}
+        w_scales = {}
+        for kp in range(PASSES):
+            for h in range(2):
+                g = keep.tile([P, 2, HALF, PACK], BF16, name="w_grp%d_%d" % (kp, h), align_bytes=64)
+                c = keep.tile([P, 2, HALF], U32, name="w_codes%d_%d" % (kp, h), align_bytes=64)
+                s = keep.tile([P, 2, HALF], U8, name="w_scales%d_%d" % (kp, h), align_bytes=64)
+                w_grp[(kp, h)] = g
+                w_codes[(kp, h)] = c
+                w_scales[(kp, h)] = s
+        x_grp = {}
+        x_codes = {}
+        x_scales = {}
+        for ch in range(chunks):
+            for kp in range(PASSES):
+                g = keep.tile([P, CHUNK, PACK], BF16, name="x_grp%d_%d" % (ch, kp), align_bytes=64)
+                c = keep.tile([P, CHUNK], U32, name="x_codes%d_%d" % (ch, kp), align_bytes=64)
+                s = keep.tile([P, CHUNK], U8, name="x_scales%d_%d" % (ch, kp), align_bytes=64)
+                x_grp[(ch, kp)] = g
+                x_codes[(ch, kp)] = c
+                x_scales[(ch, kp)] = s
+
+        def mask(kp, j0, j1):
+            nc.vector.tensor_scalar(
+                out=hi_f[kp][:, j0:j1, :].bitcast(I32), in0=w_raw[kp][:, j0:j1, :].bitcast(I32),
+                scalar1=HI_MASK, scalar2=None, op0=ALU.bitwise_and)
+
+        def hi_copy(kp, h):
+            cols = slice(h * HALF, (h + 1) * HALF)
+            nc.scalar.copy(out=packed_view(w_grp[(kp, h)][:, 0, :, :]), in_=rows_view(hi_f[kp][:, :, cols]))
+
+        def lo_sub(kp, h):
+            cols = slice(h * HALF, (h + 1) * HALF)
+            nc.vector.tensor_tensor(
+                out=packed_view(w_grp[(kp, h)][:, 1, :, :]), in0=rows_view(w_raw[kp][:, :, cols]),
+                in1=rows_view(hi_f[kp][:, :, cols]), op=ALU.subtract)
+
+        def w_quant(kp, h):
+            nc.vector.quantize_mx(
+                out=w_codes[(kp, h)][:].rearrange("p s c -> p (s c)").bitcast(FP8X4),
+                scales=w_scales[(kp, h)][:].rearrange("p s c -> p (s c)"),
+                in_=w_grp[(kp, h)][:].rearrange("p s c t -> p (s c t)"))
+
+        def x_copy(copier, ch, kp, c0=0, c1=CHUNK):
+            copier(out=packed_view(x_grp[(ch, kp)][:, c0:c1, :]), in_=rows_view(x_raw[(ch, kp)][:, :, c0:c1]))
+
+        def x_quant(ch, kp):
+            nc.vector.quantize_mx(
+                out=x_codes[(ch, kp)][:].bitcast(FP8X4), scales=x_scales[(ch, kp)][:],
+                in_=x_grp[(ch, kp)][:].rearrange("p c t -> p (c t)"))
+
+        acc = {}
+
+        def matmuls(ch, kp, m):
+            if kp == 0:
+                a = psum.tile([P, CHUNK], F32, name="acc%d_%d" % (ch, m), tag="acc%d" % ((ch % 2) * M_TILES + m))
+                acc[(ch, m)] = a
+            h = m // 2
+            for part in range(2):
+                cols = slice((m % 2) * P, (m % 2 + 1) * P)
+                nc.tensor.matmul_mx(
+                    out=acc[(ch, m)][:],
+                    lhsT=w_codes[(kp, h)][:, part, cols].bitcast(FP8X4),
+                    lhsT_scale=w_scales[(kp, h)][:, part, cols],
+                    rhs=x_codes[(ch, kp)][:].bitcast(FP8X4),
+                    rhs_scale=x_scales[(ch, kp)][:],
+                    start=(kp == 0 and part == 0), stop=(kp == PASSES - 1 and part == 1))
+
+        res = {}
+        for ch in range(chunks):
+            r = keep.tile([P, M_TILES, CHUNK], F32, name="res%d" % ch)
+            res[ch] = r
+        out_v = out.rearrange("(m p) t -> p m t", p=P)
+
+        def gelu(ch, m):
+            nc.scalar.activation(out=res[ch][:, m, :], in_=acc[(ch, m)][:], func=GELU, bias=bias[:, m:m + 1])
+
+        def store(ch, m0, m1):
+            nc.sync.dma_start(out=out_v[:, m0:m1, ch * CHUNK:(ch + 1) * CHUNK], in_=res[ch][:, m0:m1, :])
+
+        V, S = nc.vector.tensor_copy, nc.scalar.copy
+
+        mask(0, 0, 2)
+        mask(0, 2, 4)
+        hi_copy(0, 0)
+        hi_copy(0, 1)
+        nc.scalar.copy(out=bias[:], in_=bT[:, 0:M_TILES])
+        lo_sub(0, 0)
+        lo_sub(0, 1)
+        x_copy(S, 0, 0)
+        w_quant(0, 0)
+        w_quant(0, 1)
+        mask(1, 0, 4)
+        x_quant(0, 0)
+        for m in range(M_TILES):
+            matmuls(0, 0, m)
+        hi_copy(1, 0)
+        hi_copy(1, 1)
+        lo_sub(1, 0)
+        lo_sub(1, 1)
+        x_copy(S, 0, 1)
+        w_quant(1, 0)
+        w_quant(1, 1)
+        x_quant(0, 1)
+        for m in range(M_TILES):
+            matmuls(0, 1, m)
+        x_copy(S, 1, 0)
+        x_copy(V, 1, 1)
+        x_quant(1, 0)
+        for m in range(M_TILES):
+            matmuls(1, 0, m)
+        for m in range(M_TILES):
+            gelu(0, m)
+        store(0, 0, 2)
+        store(0, 2, 4)
+        x_quant(1, 1)
+        for m in range(M_TILES):
+            matmuls(1, 1, m)
+        x_copy(V, 2, 0)
+        x_quant(2, 0)
+        for m in range(M_TILES):
+            gelu(1, m)
+        store(1, 0, 2)
+        store(1, 2, 4)
+        for m in range(M_TILES):
+            matmuls(2, 0, m)
+        x_copy(V, 2, 1)
+        x_quant(2, 1)
+        for m in range(M_TILES):
+            matmuls(2, 1, m)
+            gelu(2, m)
+            store(2, m, m + 1)

@@ -12,6 +12,7 @@ CHUNK = 512
 HALF = 256
 M_TILES = M // P
 HI_MASK = -1048576
+HI_MASK_PAIR = -983056
 
 FLOPS = 2 * 2 * K * M * T
 
@@ -42,29 +43,28 @@ def tile_mix_hilo_fm_gelu_kernel(tc, w, x, b, out):
         psum = ctx.enter_context(tc.psum_pool(name="psum", bufs=1))
         ctx.enter_context(tc.manual_schedule())
 
-        w_raw = []
-        x_raw = {}
-        for kp in range(PASSES):
-            wr = keep.tile([P, PACK, M], F32, name="w_raw%d" % kp, align_bytes=64)
-            w_raw.append(wr)
+        w_raw = [keep.tile([P, PACK, M], F32, name="w_raw%d" % kp, align_bytes=64) for kp in range(PASSES)]
+        ab_raw = [keep.tile([P, PACK, 2 * CHUNK], F32, name="ab_raw%d" % kp, align_bytes=64) for kp in range(PASSES)]
+        c_raw = [keep.tile([P, PACK, CHUNK], F32, name="c_raw%d" % kp, align_bytes=64) for kp in range(PASSES)]
 
-        def load_x(ch, kp):
-            xr = keep.tile([P, PACK, CHUNK], F32, name="x_raw%d_%d" % (ch, kp), align_bytes=64)
+        def load_x(tile, kp, t0, t1):
             nc.sync.dma_start(
-                out=xr[:],
-                in_=x[kp * K_PASS:(kp + 1) * K_PASS, ch * CHUNK:(ch + 1) * CHUNK].rearrange("(p j) t -> p j t", j=PACK),
-            )
-            x_raw[(ch, kp)] = xr
+                out=tile[:],
+                in_=x[kp * K_PASS:(kp + 1) * K_PASS, t0:t1].rearrange("(p j) t -> p j t", j=PACK))
 
         w_rows = [w[kp * K_PASS:(kp + 1) * K_PASS, :].rearrange("(p j) c -> p j c", j=PACK) for kp in range(PASSES)]
         nc.sync.dma_start(out=w_raw[0][:, 0:2, :], in_=w_rows[0][:, 0:2, :])
         nc.sync.dma_start(out=w_raw[0][:, 2:4, :], in_=w_rows[0][:, 2:4, :])
-        load_x(0, 0)
+        load_x(ab_raw[0], 0, 0, 2 * CHUNK)
         nc.sync.dma_start(out=w_raw[1][:], in_=w_rows[1])
-        load_x(0, 1)
-        for ch in range(1, chunks):
-            for kp in range(PASSES):
-                load_x(ch, kp)
+        load_x(ab_raw[1], 1, 0, 2 * CHUNK)
+        load_x(c_raw[0], 0, 2 * CHUNK, T)
+        load_x(c_raw[1], 1, 2 * CHUNK, T)
+        x_raw = {}
+        for kp in range(PASSES):
+            x_raw[(0, kp)] = ab_raw[kp][:, :, 0:CHUNK]
+            x_raw[(1, kp)] = ab_raw[kp][:, :, CHUNK:2 * CHUNK]
+            x_raw[(2, kp)] = c_raw[kp][:]
 
         warm = keep.tile([P, 1], F32, name="warm")
         warm_out = keep.tile([P, 1], F32, name="warm_out")
@@ -74,10 +74,9 @@ def tile_mix_hilo_fm_gelu_kernel(tc, w, x, b, out):
         nc.vector.memset(warm[:], 0.0)
         nc.gpsimd.memset(b_rows[:], 0.0)
         make_identity(nc, ident[:])
-        nc.scalar.activation(out=warm_out[:], in_=warm[:], func=GELU)
         nc.scalar.dma_start(out=b_rows[0:M_TILES, :], in_=b.rearrange("(m p) -> m p", p=P))
+        nc.scalar.activation(out=warm_out[:], in_=warm[:], func=GELU)
         bT = psum.tile([P, CHUNK], F32, name="bT", tag="acc7")
-        nc.tensor.transpose(bT[:, 0:P], b_rows[:], ident[:])
 
         hi_f = [keep.tile([P, PACK, M], F32, name="hi_f%d" % kp, align_bytes=64) for kp in range(PASSES)]
         w_grp = {}
@@ -103,9 +102,9 @@ def tile_mix_hilo_fm_gelu_kernel(tc, w, x, b, out):
                 x_codes[(ch, kp)] = c
                 x_scales[(ch, kp)] = s
 
-        def mask(kp, j0, j1):
+        def mask(kp, j0, j1, c0=0, c1=M):
             nc.vector.tensor_scalar(
-                out=hi_f[kp][:, j0:j1, :].bitcast(I32), in0=w_raw[kp][:, j0:j1, :].bitcast(I32),
+                out=hi_f[kp][:, j0:j1, c0:c1].bitcast(I32), in0=w_raw[kp][:, j0:j1, c0:c1].bitcast(I32),
                 scalar1=HI_MASK, scalar2=None, op0=ALU.bitwise_and)
 
         def hi_copy(kp, h):
@@ -117,6 +116,20 @@ def tile_mix_hilo_fm_gelu_kernel(tc, w, x, b, out):
             nc.vector.tensor_tensor(
                 out=packed_view(w_grp[(kp, h)][:, 1, :, :]), in0=rows_view(w_raw[kp][:, :, cols]),
                 in1=rows_view(hi_f[kp][:, :, cols]), op=ALU.subtract)
+
+        def trunc_copy(h):
+            top = w_raw[1][:].bitcast(BF16)[:, :, 2 * h * HALF + 1:2 * (h + 1) * HALF:2]
+            nc.scalar.copy(out=packed_view(w_grp[(1, h)][:, 0, :, :]), in_=rows_view(top))
+
+        def mask_pairs(h):
+            words = w_grp[(1, h)][:, 0, :, :].rearrange("p c t -> p (c t)").bitcast(I32)
+            nc.vector.tensor_scalar(out=words, in0=words, scalar1=HI_MASK_PAIR, scalar2=None, op0=ALU.bitwise_and)
+
+        def lo_sub_packed(h):
+            cols = slice(h * HALF, (h + 1) * HALF)
+            nc.vector.tensor_tensor(
+                out=packed_view(w_grp[(1, h)][:, 1, :, :]), in0=rows_view(w_raw[1][:, :, cols]),
+                in1=packed_view(w_grp[(1, h)][:, 0, :, :]), op=ALU.subtract)
 
         def w_quant(kp, h):
             nc.vector.quantize_mx(
@@ -131,6 +144,17 @@ def tile_mix_hilo_fm_gelu_kernel(tc, w, x, b, out):
             nc.vector.quantize_mx(
                 out=x_codes[(ch, kp)][:].bitcast(FP8X4), scales=x_scales[(ch, kp)][:],
                 in_=x_grp[(ch, kp)][:].rearrange("p c t -> p (c t)"))
+
+        def warm_up(passes):
+            scratch = psum.tile([P, CHUNK], F32, name="scratch", tag="acc6")
+            for i in range(passes):
+                nc.tensor.matmul_mx(
+                    out=scratch[:],
+                    lhsT=w_codes[(0, 0)][:, 0, 0:P].bitcast(FP8X4),
+                    lhsT_scale=w_scales[(0, 0)][:, 0, 0:P],
+                    rhs=w_codes[(0, 0)][:].rearrange("p s c -> p (s c)").bitcast(FP8X4),
+                    rhs_scale=w_scales[(0, 0)][:].rearrange("p s c -> p (s c)"),
+                    start=True, stop=True)
 
         acc = {}
 
@@ -167,49 +191,61 @@ def tile_mix_hilo_fm_gelu_kernel(tc, w, x, b, out):
         mask(0, 2, 4)
         hi_copy(0, 0)
         hi_copy(0, 1)
-        nc.scalar.copy(out=bias[:], in_=bT[:, 0:M_TILES])
         lo_sub(0, 0)
         lo_sub(0, 1)
-        x_copy(S, 0, 0)
         w_quant(0, 0)
+        warm_up(5)
+        nc.tensor.transpose(bT[:, 0:P], b_rows[:], ident[:])
         w_quant(0, 1)
-        mask(1, 0, 4)
+        x_copy(V, 0, 0, 0, HALF)
+        x_copy(S, 0, 0, HALF, CHUNK)
+        x_copy(V, 1, 0, 0, HALF)
+        x_copy(S, 1, 0, HALF, CHUNK)
+        nc.scalar.copy(out=bias[:], in_=bT[:, 0:M_TILES])
         x_quant(0, 0)
         for m in range(M_TILES):
             matmuls(0, 0, m)
-        hi_copy(1, 0)
-        hi_copy(1, 1)
-        lo_sub(1, 0)
-        lo_sub(1, 1)
-        x_copy(S, 0, 1)
-        w_quant(1, 0)
-        w_quant(1, 1)
-        x_quant(0, 1)
-        for m in range(M_TILES):
-            matmuls(0, 1, m)
-        x_copy(S, 1, 0)
-        x_copy(V, 1, 1)
+        mask(1, 0, 4, 0, HALF)
         x_quant(1, 0)
         for m in range(M_TILES):
             matmuls(1, 0, m)
+        trunc_copy(1)
+        hi_copy(1, 0)
+        lo_sub(1, 0)
+        mask_pairs(1)
+        w_quant(1, 0)
+        lo_sub_packed(1)
+        x_copy(S, 0, 1, HALF, CHUNK)
+        x_copy(V, 0, 1, 0, HALF)
+        x_copy(S, 1, 1, HALF, CHUNK)
+        x_copy(V, 1, 1, 0, HALF)
+        x_quant(0, 1)
+        matmuls(0, 1, 0)
+        matmuls(0, 1, 1)
+        w_quant(1, 1)
+        matmuls(0, 1, 2)
+        matmuls(0, 1, 3)
+        x_copy(S, 2, 0, HALF, CHUNK)
+        x_copy(V, 2, 0, 0, HALF)
+        x_quant(1, 1)
+        for m in range(M_TILES):
+            matmuls(1, 1, m)
         for m in range(M_TILES):
             gelu(0, m)
         store(0, 0, 2)
         store(0, 2, 4)
-        x_quant(1, 1)
-        for m in range(M_TILES):
-            matmuls(1, 1, m)
-        x_copy(V, 2, 0)
         x_quant(2, 0)
+        for m in range(M_TILES):
+            matmuls(2, 0, m)
         for m in range(M_TILES):
             gelu(1, m)
         store(1, 0, 2)
         store(1, 2, 4)
-        for m in range(M_TILES):
-            matmuls(2, 0, m)
-        x_copy(V, 2, 1)
+        x_copy(V, 2, 1, 0, HALF)
+        x_copy(V, 2, 1, HALF, CHUNK)
         x_quant(2, 1)
         for m in range(M_TILES):
             matmuls(2, 1, m)
             gelu(2, m)
-            store(2, m, m + 1)
+            if m % 2 == 1:
+                store(2, m - 1, m + 1)

@@ -11,6 +11,7 @@ PASSES = K // K_PASS
 CHUNK = 512
 HALF = 256
 M_TILES = M // P
+GROUPS = [(0, 0, CHUNK), (1, 0, CHUNK), (2, 0, HALF), (2, HALF, CHUNK)]
 HI_MASK = -1048576
 HI_MASK_PAIR = -983056
 
@@ -44,7 +45,9 @@ def tile_mix_hilo_fm_gelu_kernel(tc, w, x, b, out):
         ctx.enter_context(tc.manual_schedule())
 
         w_raw = [keep.tile([P, PACK, M], F32, name="w_raw%d" % kp, align_bytes=64) for kp in range(PASSES)]
-        ab_raw = [keep.tile([P, PACK, 2 * CHUNK], F32, name="ab_raw%d" % kp, align_bytes=64) for kp in range(PASSES)]
+        ab0 = keep.tile([P, PACK, 2 * CHUNK], F32, name="ab0", align_bytes=64)
+        a1 = keep.tile([P, PACK, CHUNK], F32, name="a1", align_bytes=64)
+        b1 = keep.tile([P, PACK, CHUNK], F32, name="b1", align_bytes=64)
         c_raw = [keep.tile([P, PACK, CHUNK], F32, name="c_raw%d" % kp, align_bytes=64) for kp in range(PASSES)]
 
         def load_x(tile, kp, t0, t1):
@@ -55,16 +58,16 @@ def tile_mix_hilo_fm_gelu_kernel(tc, w, x, b, out):
         w_rows = [w[kp * K_PASS:(kp + 1) * K_PASS, :].rearrange("(p j) c -> p j c", j=PACK) for kp in range(PASSES)]
         nc.sync.dma_start(out=w_raw[0][:, 0:2, :], in_=w_rows[0][:, 0:2, :])
         nc.sync.dma_start(out=w_raw[0][:, 2:4, :], in_=w_rows[0][:, 2:4, :])
-        load_x(ab_raw[0], 0, 0, 2 * CHUNK)
+        load_x(ab0, 0, 0, 2 * CHUNK)
         nc.sync.dma_start(out=w_raw[1][:], in_=w_rows[1])
-        load_x(ab_raw[1], 1, 0, 2 * CHUNK)
+        load_x(a1, 1, 0, CHUNK)
+        load_x(b1, 1, CHUNK, 2 * CHUNK)
         load_x(c_raw[0], 0, 2 * CHUNK, T)
         load_x(c_raw[1], 1, 2 * CHUNK, T)
-        x_raw = {}
-        for kp in range(PASSES):
-            x_raw[(0, kp)] = ab_raw[kp][:, :, 0:CHUNK]
-            x_raw[(1, kp)] = ab_raw[kp][:, :, CHUNK:2 * CHUNK]
-            x_raw[(2, kp)] = c_raw[kp][:]
+        x_raw = {
+            (0, 0): ab0[:, :, 0:CHUNK], (1, 0): ab0[:, :, CHUNK:2 * CHUNK],
+            (0, 1): a1[:], (1, 1): b1[:], (2, 0): c_raw[0][:], (2, 1): c_raw[1][:],
+        }
 
         warm = keep.tile([P, 1], F32, name="warm")
         warm_out = keep.tile([P, 1], F32, name="warm_out")
@@ -107,9 +110,9 @@ def tile_mix_hilo_fm_gelu_kernel(tc, w, x, b, out):
                 out=hi_f[kp][:, j0:j1, c0:c1].bitcast(I32), in0=w_raw[kp][:, j0:j1, c0:c1].bitcast(I32),
                 scalar1=HI_MASK, scalar2=None, op0=ALU.bitwise_and)
 
-        def hi_copy(kp, h):
+        def hi_copy(copier, kp, h):
             cols = slice(h * HALF, (h + 1) * HALF)
-            nc.scalar.copy(out=packed_view(w_grp[(kp, h)][:, 0, :, :]), in_=rows_view(hi_f[kp][:, :, cols]))
+            copier(out=packed_view(w_grp[(kp, h)][:, 0, :, :]), in_=rows_view(hi_f[kp][:, :, cols]))
 
         def lo_sub(kp, h):
             cols = slice(h * HALF, (h + 1) * HALF)
@@ -140,10 +143,10 @@ def tile_mix_hilo_fm_gelu_kernel(tc, w, x, b, out):
         def x_copy(copier, ch, kp, c0=0, c1=CHUNK):
             copier(out=packed_view(x_grp[(ch, kp)][:, c0:c1, :]), in_=rows_view(x_raw[(ch, kp)][:, :, c0:c1]))
 
-        def x_quant(ch, kp):
+        def x_quant(ch, kp, c0=0, c1=CHUNK):
             nc.vector.quantize_mx(
-                out=x_codes[(ch, kp)][:].bitcast(FP8X4), scales=x_scales[(ch, kp)][:],
-                in_=x_grp[(ch, kp)][:].rearrange("p c t -> p (c t)"))
+                out=x_codes[(ch, kp)][:, c0:c1].bitcast(FP8X4), scales=x_scales[(ch, kp)][:, c0:c1],
+                in_=x_grp[(ch, kp)][:, c0:c1, :].rearrange("p c t -> p (c t)"))
 
         def warm_up(passes):
             scratch = psum.tile([P, CHUNK], F32, name="scratch", tag="acc6")
@@ -158,19 +161,20 @@ def tile_mix_hilo_fm_gelu_kernel(tc, w, x, b, out):
 
         acc = {}
 
-        def matmuls(ch, kp, m):
+        def matmuls(group, kp, m):
+            ch, c0, c1 = GROUPS[group]
             if kp == 0:
-                a = psum.tile([P, CHUNK], F32, name="acc%d_%d" % (ch, m), tag="acc%d" % ((ch % 2) * M_TILES + m))
-                acc[(ch, m)] = a
+                a = psum.tile([P, c1 - c0], F32, name="acc%d_%d" % (group, m), tag="acc%d" % ((group % 2) * M_TILES + m))
+                acc[(group, m)] = a
             h = m // 2
             for part in range(2):
                 cols = slice((m % 2) * P, (m % 2 + 1) * P)
                 nc.tensor.matmul_mx(
-                    out=acc[(ch, m)][:],
+                    out=acc[(group, m)][:],
                     lhsT=w_codes[(kp, h)][:, part, cols].bitcast(FP8X4),
                     lhsT_scale=w_scales[(kp, h)][:, part, cols],
-                    rhs=x_codes[(ch, kp)][:].bitcast(FP8X4),
-                    rhs_scale=x_scales[(ch, kp)][:],
+                    rhs=x_codes[(ch, kp)][:, c0:c1].bitcast(FP8X4),
+                    rhs_scale=x_scales[(ch, kp)][:, c0:c1],
                     start=(kp == 0 and part == 0), stop=(kp == PASSES - 1 and part == 1))
 
         res = {}
@@ -179,18 +183,21 @@ def tile_mix_hilo_fm_gelu_kernel(tc, w, x, b, out):
             res[ch] = r
         out_v = out.rearrange("(m p) t -> p m t", p=P)
 
-        def gelu(ch, m):
-            nc.scalar.activation(out=res[ch][:, m, :], in_=acc[(ch, m)][:], func=GELU, bias=bias[:, m:m + 1])
+        def gelu(group, m):
+            ch, c0, c1 = GROUPS[group]
+            nc.scalar.activation(out=res[ch][:, m, c0:c1], in_=acc[(group, m)][:], func=GELU, bias=bias[:, m:m + 1])
 
-        def store(ch, m0, m1):
-            nc.sync.dma_start(out=out_v[:, m0:m1, ch * CHUNK:(ch + 1) * CHUNK], in_=res[ch][:, m0:m1, :])
+        def store(group, m0, m1):
+            ch, c0, c1 = GROUPS[group]
+            nc.sync.dma_start(
+                out=out_v[:, m0:m1, ch * CHUNK + c0:ch * CHUNK + c1], in_=res[ch][:, m0:m1, c0:c1])
 
         V, S = nc.vector.tensor_copy, nc.scalar.copy
 
         mask(0, 0, 2)
         mask(0, 2, 4)
-        hi_copy(0, 0)
-        hi_copy(0, 1)
+        hi_copy(S, 0, 0)
+        hi_copy(V, 0, 1)
         lo_sub(0, 0)
         lo_sub(0, 1)
         w_quant(0, 0)
@@ -210,23 +217,21 @@ def tile_mix_hilo_fm_gelu_kernel(tc, w, x, b, out):
         for m in range(M_TILES):
             matmuls(1, 0, m)
         trunc_copy(1)
-        hi_copy(1, 0)
+        hi_copy(S, 1, 0)
         lo_sub(1, 0)
         mask_pairs(1)
-        w_quant(1, 0)
-        lo_sub_packed(1)
         x_copy(S, 0, 1, HALF, CHUNK)
         x_copy(V, 0, 1, 0, HALF)
-        x_copy(S, 1, 1, HALF, CHUNK)
-        x_copy(V, 1, 1, 0, HALF)
+        lo_sub_packed(1)
+        w_quant(1, 0)
         x_quant(0, 1)
         matmuls(0, 1, 0)
         matmuls(0, 1, 1)
         w_quant(1, 1)
         matmuls(0, 1, 2)
         matmuls(0, 1, 3)
-        x_copy(S, 2, 0, HALF, CHUNK)
-        x_copy(V, 2, 0, 0, HALF)
+        x_copy(S, 1, 1, HALF, CHUNK)
+        x_copy(V, 1, 1, 0, HALF)
         x_quant(1, 1)
         for m in range(M_TILES):
             matmuls(1, 1, m)
@@ -234,18 +239,29 @@ def tile_mix_hilo_fm_gelu_kernel(tc, w, x, b, out):
             gelu(0, m)
         store(0, 0, 2)
         store(0, 2, 4)
+        x_copy(V, 2, 0)
         x_quant(2, 0)
         for m in range(M_TILES):
             matmuls(2, 0, m)
-        for m in range(M_TILES):
-            gelu(1, m)
+        gelu(1, 0)
+        gelu(1, 1)
         store(1, 0, 2)
-        store(1, 2, 4)
+        gelu(1, 2)
         x_copy(V, 2, 1, 0, HALF)
-        x_copy(V, 2, 1, HALF, CHUNK)
-        x_quant(2, 1)
+        x_copy(S, 2, 1, HALF + P, CHUNK)
+        x_copy(V, 2, 1, HALF, HALF + P)
+        x_quant(2, 1, 0, HALF)
+        gelu(1, 3)
+        store(1, 2, 4)
+        x_quant(2, 1, HALF, CHUNK)
+        for m in range(M_TILES):
+            matmuls(3, 0, m)
         for m in range(M_TILES):
             matmuls(2, 1, m)
             gelu(2, m)
+        store(2, 0, 4)
+        for m in range(M_TILES):
+            matmuls(3, 1, m)
+            gelu(3, m)
             if m % 2 == 1:
-                store(2, m - 1, m + 1)
+                store(3, m - 1, m + 1)

@@ -45,9 +45,8 @@ def tile_mix_hilo_fm_gelu_kernel(tc, w, x, b, out):
         ctx.enter_context(tc.manual_schedule())
 
         w_raw = [keep.tile([P, PACK, M], F32, name="w_raw%d" % kp, align_bytes=64) for kp in range(PASSES)]
-        ab0 = keep.tile([P, PACK, 2 * CHUNK], F32, name="ab0", align_bytes=64)
-        a1 = keep.tile([P, PACK, CHUNK], F32, name="a1", align_bytes=64)
-        b1 = keep.tile([P, PACK, CHUNK], F32, name="b1", align_bytes=64)
+        a_raw = [keep.tile([P, PACK, CHUNK], F32, name="a_raw%d" % kp, align_bytes=64) for kp in range(PASSES)]
+        b_raw = [keep.tile([P, PACK, CHUNK], F32, name="b_raw%d" % kp, align_bytes=64) for kp in range(PASSES)]
         c_raw = [keep.tile([P, PACK, CHUNK], F32, name="c_raw%d" % kp, align_bytes=64) for kp in range(PASSES)]
 
         def load_x(tile, kp, t0, t1):
@@ -58,16 +57,14 @@ def tile_mix_hilo_fm_gelu_kernel(tc, w, x, b, out):
         w_rows = [w[kp * K_PASS:(kp + 1) * K_PASS, :].rearrange("(p j) c -> p j c", j=PACK) for kp in range(PASSES)]
         nc.sync.dma_start(out=w_raw[0][:, 0:2, :], in_=w_rows[0][:, 0:2, :])
         nc.sync.dma_start(out=w_raw[0][:, 2:4, :], in_=w_rows[0][:, 2:4, :])
-        load_x(ab0, 0, 0, 2 * CHUNK)
+        load_x(a_raw[0], 0, 0, CHUNK)
         nc.sync.dma_start(out=w_raw[1][:], in_=w_rows[1])
-        load_x(a1, 1, 0, CHUNK)
-        load_x(b1, 1, CHUNK, 2 * CHUNK)
+        load_x(b_raw[0], 0, CHUNK, 2 * CHUNK)
+        load_x(a_raw[1], 1, 0, CHUNK)
+        load_x(b_raw[1], 1, CHUNK, 2 * CHUNK)
         load_x(c_raw[0], 0, 2 * CHUNK, T)
         load_x(c_raw[1], 1, 2 * CHUNK, T)
-        x_raw = {
-            (0, 0): ab0[:, :, 0:CHUNK], (1, 0): ab0[:, :, CHUNK:2 * CHUNK],
-            (0, 1): a1[:], (1, 1): b1[:], (2, 0): c_raw[0][:], (2, 1): c_raw[1][:],
-        }
+        x_raw = {(ch, kp): tile[:] for kp in range(PASSES) for ch, tile in enumerate((a_raw[kp], b_raw[kp], c_raw[kp]))}
 
         warm = keep.tile([P, 1], F32, name="warm")
         warm_out = keep.tile([P, 1], F32, name="warm_out")
@@ -197,33 +194,33 @@ def tile_mix_hilo_fm_gelu_kernel(tc, w, x, b, out):
         mask(0, 0, 2)
         mask(0, 2, 4)
         hi_copy(S, 0, 0)
-        hi_copy(V, 0, 1)
+        hi_copy(S, 0, 1)
         lo_sub(0, 0)
         lo_sub(0, 1)
         w_quant(0, 0)
-        warm_up(5)
+        warm_up(4)
         nc.tensor.transpose(bT[:, 0:P], b_rows[:], ident[:])
-        w_quant(0, 1)
-        x_copy(V, 0, 0, 0, HALF)
         x_copy(S, 0, 0, HALF, CHUNK)
-        x_copy(V, 1, 0, 0, HALF)
-        x_copy(S, 1, 0, HALF, CHUNK)
-        nc.scalar.copy(out=bias[:], in_=bT[:, 0:M_TILES])
+        x_copy(V, 0, 0, 0, HALF)
+        w_quant(0, 1)
+        mask(1, 0, 4, 0, HALF)
         x_quant(0, 0)
         for m in range(M_TILES):
             matmuls(0, 0, m)
-        mask(1, 0, 4, 0, HALF)
-        x_quant(1, 0)
-        for m in range(M_TILES):
-            matmuls(1, 0, m)
         trunc_copy(1)
         hi_copy(S, 1, 0)
         lo_sub(1, 0)
+        x_copy(S, 1, 0, HALF, CHUNK)
+        x_copy(V, 1, 0, 0, HALF)
+        w_quant(1, 0)
+        nc.scalar.copy(out=bias[:], in_=bT[:, 0:M_TILES])
+        x_quant(1, 0)
+        for m in range(M_TILES):
+            matmuls(1, 0, m)
         mask_pairs(1)
         x_copy(S, 0, 1, HALF, CHUNK)
         x_copy(V, 0, 1, 0, HALF)
         lo_sub_packed(1)
-        w_quant(1, 0)
         x_quant(0, 1)
         matmuls(0, 1, 0)
         matmuls(0, 1, 1)
@@ -255,13 +252,14 @@ def tile_mix_hilo_fm_gelu_kernel(tc, w, x, b, out):
         store(1, 2, 4)
         x_quant(2, 1, HALF, CHUNK)
         for m in range(M_TILES):
-            matmuls(3, 0, m)
-        for m in range(M_TILES):
             matmuls(2, 1, m)
             gelu(2, m)
         store(2, 0, 4)
         for m in range(M_TILES):
+            matmuls(3, 0, m)
             matmuls(3, 1, m)
             gelu(3, m)
-            if m % 2 == 1:
-                store(3, m - 1, m + 1)
+            if m == 1:
+                store(3, 0, 2)
+            if m > 1:
+                store(3, m, m + 1)

from contextlib import ExitStack

import concourse.mybir as mybir
from concourse.masks import make_identity

K, M, T = 1024, 512, 1536
P = 128
PACK = 4
K_PASS = P * PACK
PASSES = K // K_PASS
CHUNK = 512
HALF = 256
M_TILES = M // P
GROUPS = [(0, 0, CHUNK), (1, 0, CHUNK), (2, 0, HALF), (2, HALF, CHUNK)]
HI_MASK = -1048576
HI_MASK_PAIR = -983056

FLOPS = 2 * 2 * K * M * T

F32 = mybir.dt.float32
BF16 = mybir.dt.bfloat16
I32 = mybir.dt.int32
U32 = mybir.dt.uint32
U8 = mybir.dt.uint8
FP8X4 = mybir.dt.float8_e4m3fn_x4
ALU = mybir.AluOpType
GELU = mybir.ActivationFunctionType.Gelu_apprx_tanh


def rows_view(raw):
    return raw.rearrange("p t (c i) -> p c t i", i=4)


def packed_view(grouped):
    return grouped.rearrange("p (c i) t -> p c t i", i=4)


def tile_mix_hilo_fm_gelu_kernel(tc, w, x, b, out):
    nc = tc.nc
    chunks = T // CHUNK

    with ExitStack() as ctx:
        keep = ctx.enter_context(tc.tile_pool(name="keep", bufs=1))
        psum = ctx.enter_context(tc.psum_pool(name="psum", bufs=1))
        ctx.enter_context(tc.manual_schedule())

        w_raw = [keep.tile([P, PACK, M], F32, name="w_raw%d" % kp, align_bytes=64) for kp in range(PASSES)]
        a_raw = [keep.tile([P, PACK, CHUNK], F32, name="a_raw%d" % kp, align_bytes=64) for kp in range(PASSES)]
        b_raw = [keep.tile([P, PACK, CHUNK], F32, name="b_raw%d" % kp, align_bytes=64) for kp in range(PASSES)]
        c_raw = [keep.tile([P, PACK, CHUNK], F32, name="c_raw%d" % kp, align_bytes=64) for kp in range(PASSES)]

        def load_x(tile, kp, t0, t1):
            nc.sync.dma_start(
                out=tile[:],
                in_=x[kp * K_PASS:(kp + 1) * K_PASS, t0:t1].rearrange("(p j) t -> p j t", j=PACK))

        w_rows = [w[kp * K_PASS:(kp + 1) * K_PASS, :].rearrange("(p j) c -> p j c", j=PACK) for kp in range(PASSES)]
        nc.sync.dma_start(out=w_raw[0][:, 0:2, :], in_=w_rows[0][:, 0:2, :])
        nc.sync.dma_start(out=w_raw[0][:, 2:4, :], in_=w_rows[0][:, 2:4, :])
        load_x(a_raw[0], 0, 0, CHUNK)
        nc.sync.dma_start(out=w_raw[1][:], in_=w_rows[1])
        load_x(b_raw[0], 0, CHUNK, 2 * CHUNK)
        load_x(a_raw[1], 1, 0, CHUNK)
        load_x(b_raw[1], 1, CHUNK, 2 * CHUNK)
        load_x(c_raw[0], 0, 2 * CHUNK, T)
        load_x(c_raw[1], 1, 2 * CHUNK, T)
        x_raw = {(ch, kp): tile[:] for kp in range(PASSES) for ch, tile in enumerate((a_raw[kp], b_raw[kp], c_raw[kp]))}

        warm = keep.tile([P, 1], F32, name="warm")
        warm_out = keep.tile([P, 1], F32, name="warm_out")
        b_rows = keep.tile([P, P], F32, name="b_rows")
        ident = keep.tile([P, P], F32, name="ident")
        bias = keep.tile([P, M_TILES], F32, name="bias")
        nc.vector.memset(warm[:], 0.0)
        nc.gpsimd.memset(b_rows[:], 0.0)
        make_identity(nc, ident[:])
        nc.scalar.dma_start(out=b_rows[0:M_TILES, :], in_=b.rearrange("(m p) -> m p", p=P))
        nc.scalar.activation(out=warm_out[:], in_=warm[:], func=GELU)
        bT = psum.tile([P, CHUNK], F32, name="bT", tag="acc7")

        hi_f = [keep.tile([P, PACK, M], F32, name="hi_f%d" % kp, align_bytes=64) for kp in range(PASSES)]
        w_grp = {}
        w_codes = {}
        w_scales = {}
        for kp in range(PASSES):
            for h in range(2):
                g = keep.tile([P, 2, HALF, PACK], BF16, name="w_grp%d_%d" % (kp, h), align_bytes=64)
                c = keep.tile([P, 2, HALF], U32, name="w_codes%d_%d" % (kp, h), align_bytes=64)
                s = keep.tile([P, 2, HALF], U8, name="w_scales%d_%d" % (kp, h), align_bytes=64)
                w_grp[(kp, h)] = g
                w_codes[(kp, h)] = c
                w_scales[(kp, h)] = s
        x_grp = {}
        x_codes = {}
        x_scales = {}
        for ch in range(chunks):
            for kp in range(PASSES):
                g = keep.tile([P, CHUNK, PACK], BF16, name="x_grp%d_%d" % (ch, kp), align_bytes=64)
                c = keep.tile([P, CHUNK], U32, name="x_codes%d_%d" % (ch, kp), align_bytes=64)
                s = keep.tile([P, CHUNK], U8, name="x_scales%d_%d" % (ch, kp), align_bytes=64)
                x_grp[(ch, kp)] = g
                x_codes[(ch, kp)] = c
                x_scales[(ch, kp)] = s

        def mask(kp, j0, j1, c0=0, c1=M):
            nc.vector.tensor_scalar(
                out=hi_f[kp][:, j0:j1, c0:c1].bitcast(I32), in0=w_raw[kp][:, j0:j1, c0:c1].bitcast(I32),
                scalar1=HI_MASK, scalar2=None, op0=ALU.bitwise_and)

        def hi_copy(copier, kp, h):
            cols = slice(h * HALF, (h + 1) * HALF)
            copier(out=packed_view(w_grp[(kp, h)][:, 0, :, :]), in_=rows_view(hi_f[kp][:, :, cols]))

        def lo_sub(kp, h):
            cols = slice(h * HALF, (h + 1) * HALF)
            nc.vector.tensor_tensor(
                out=packed_view(w_grp[(kp, h)][:, 1, :, :]), in0=rows_view(w_raw[kp][:, :, cols]),
                in1=rows_view(hi_f[kp][:, :, cols]), op=ALU.subtract)

        def trunc_copy(h):
            top = w_raw[1][:].bitcast(BF16)[:, :, 2 * h * HALF + 1:2 * (h + 1) * HALF:2]
            nc.scalar.copy(out=packed_view(w_grp[(1, h)][:, 0, :, :]), in_=rows_view(top))

        def mask_pairs(h):
            words = w_grp[(1, h)][:, 0, :, :].rearrange("p c t -> p (c t)").bitcast(I32)
            nc.vector.tensor_scalar(out=words, in0=words, scalar1=HI_MASK_PAIR, scalar2=None, op0=ALU.bitwise_and)

        def lo_sub_packed(h):
            cols = slice(h * HALF, (h + 1) * HALF)
            nc.vector.tensor_tensor(
                out=packed_view(w_grp[(1, h)][:, 1, :, :]), in0=rows_view(w_raw[1][:, :, cols]),
                in1=packed_view(w_grp[(1, h)][:, 0, :, :]), op=ALU.subtract)

        def w_quant(kp, h):
            nc.vector.quantize_mx(
                out=w_codes[(kp, h)][:].rearrange("p s c -> p (s c)").bitcast(FP8X4),
                scales=w_scales[(kp, h)][:].rearrange("p s c -> p (s c)"),
                in_=w_grp[(kp, h)][:].rearrange("p s c t -> p (s c t)"))

        def x_copy(copier, ch, kp, c0=0, c1=CHUNK):
            copier(out=packed_view(x_grp[(ch, kp)][:, c0:c1, :]), in_=rows_view(x_raw[(ch, kp)][:, :, c0:c1]))

        def x_quant(ch, kp, c0=0, c1=CHUNK):
            nc.vector.quantize_mx(
                out=x_codes[(ch, kp)][:, c0:c1].bitcast(FP8X4), scales=x_scales[(ch, kp)][:, c0:c1],
                in_=x_grp[(ch, kp)][:, c0:c1, :].rearrange("p c t -> p (c t)"))

        def warm_up(passes):
            scratch = psum.tile([P, CHUNK], F32, name="scratch", tag="acc6")
            for i in range(passes):
                nc.tensor.matmul_mx(
                    out=scratch[:],
                    lhsT=w_codes[(0, 0)][:, 0, 0:P].bitcast(FP8X4),
                    lhsT_scale=w_scales[(0, 0)][:, 0, 0:P],
                    rhs=w_codes[(0, 0)][:].rearrange("p s c -> p (s c)").bitcast(FP8X4),
                    rhs_scale=w_scales[(0, 0)][:].rearrange("p s c -> p (s c)"),
                    start=True, stop=True)

        acc = {}

        def matmuls(group, kp, m):
            ch, c0, c1 = GROUPS[group]
            if kp == 0:
                a = psum.tile([P, c1 - c0], F32, name="acc%d_%d" % (group, m), tag="acc%d" % ((group % 2) * M_TILES + m))
                acc[(group, m)] = a
            h = m // 2
            for part in range(2):
                cols = slice((m % 2) * P, (m % 2 + 1) * P)
                nc.tensor.matmul_mx(
                    out=acc[(group, m)][:],
                    lhsT=w_codes[(kp, h)][:, part, cols].bitcast(FP8X4),
                    lhsT_scale=w_scales[(kp, h)][:, part, cols],
                    rhs=x_codes[(ch, kp)][:, c0:c1].bitcast(FP8X4),
                    rhs_scale=x_scales[(ch, kp)][:, c0:c1],
                    start=(kp == 0 and part == 0), stop=(kp == PASSES - 1 and part == 1))

        res = {}
        for ch in range(chunks):
            r = keep.tile([P, M_TILES, CHUNK], F32, name="res%d" % ch)
            res[ch] = r
        out_v = out.rearrange("(m p) t -> p m t", p=P)

        def gelu(group, m):
            ch, c0, c1 = GROUPS[group]
            nc.scalar.activation(out=res[ch][:, m, c0:c1], in_=acc[(group, m)][:], func=GELU, bias=bias[:, m:m + 1])

        def store(group, m0, m1):
            ch, c0, c1 = GROUPS[group]
            nc.sync.dma_start(
                out=out_v[:, m0:m1, ch * CHUNK + c0:ch * CHUNK + c1], in_=res[ch][:, m0:m1, c0:c1])

        V, S = nc.vector.tensor_copy, nc.scalar.copy

        mask(0, 0, 2)
        mask(0, 2, 4)
        hi_copy(S, 0, 0)
        hi_copy(S, 0, 1)
        lo_sub(0, 0)
        lo_sub(0, 1)
        w_quant(0, 0)
        warm_up(4)
        nc.tensor.transpose(bT[:, 0:P], b_rows[:], ident[:])
        x_copy(S, 0, 0, HALF, CHUNK)
        x_copy(V, 0, 0, 0, HALF)
        w_quant(0, 1)
        mask(1, 0, 4, 0, HALF)
        x_quant(0, 0)
        for m in range(M_TILES):
            matmuls(0, 0, m)
        trunc_copy(1)
        hi_copy(S, 1, 0)
        lo_sub(1, 0)
        x_copy(S, 1, 0, HALF, CHUNK)
        x_copy(V, 1, 0, 0, HALF)
        w_quant(1, 0)
        nc.scalar.copy(out=bias[:], in_=bT[:, 0:M_TILES])
        x_quant(1, 0)
        for m in range(M_TILES):
            matmuls(1, 0, m)
        mask_pairs(1)
        x_copy(S, 0, 1, HALF, CHUNK)
        x_copy(V, 0, 1, 0, HALF)
        lo_sub_packed(1)
        x_quant(0, 1)
        matmuls(0, 1, 0)
        matmuls(0, 1, 1)
        w_quant(1, 1)
        matmuls(0, 1, 2)
        matmuls(0, 1, 3)
        x_copy(S, 1, 1, HALF, CHUNK)
        x_copy(V, 1, 1, 0, HALF)
        x_quant(1, 1)
        for m in range(M_TILES):
            matmuls(1, 1, m)
        for m in range(M_TILES):
            gelu(0, m)
        store(0, 0, 2)
        store(0, 2, 4)
        x_copy(V, 2, 0)
        x_quant(2, 0)
        for m in range(M_TILES):
            matmuls(2, 0, m)
        gelu(1, 0)
        gelu(1, 1)
        store(1, 0, 2)
        gelu(1, 2)
        x_copy(V, 2, 1, 0, HALF)
        x_copy(S, 2, 1, HALF + P, CHUNK)
        x_copy(V, 2, 1, HALF, HALF + P)
        x_quant(2, 1, 0, HALF)
        gelu(1, 3)
        store(1, 2, 4)
        x_quant(2, 1, HALF, CHUNK)
        for m in range(M_TILES):
            matmuls(2, 1, m)
            gelu(2, m)
        store(2, 0, 4)
        for m in range(M_TILES):
            matmuls(3, 0, m)
            matmuls(3, 1, m)
            gelu(3, m)
            if m == 1:
                store(3, 0, 2)
            if m > 1:
                store(3, m, m + 1)
